import numpy as np, ml_dtypes
CORES = [168,169,170,171,172,296,424,40]
N = 8
import mx_ref
NC, KB = 128, 1
BF = ml_dtypes.bfloat16
def cut(t, i, w=512):
    return t[:, w * i:w * i + w]
def term(a, B):
    return np.stack([mx_ref.matmul(mx_ref.quantize(cut(a, i)), B) for i in range(4)], axis=2).reshape(128, -1)
def setup_inputs(rng):
    def f(*shape):
        return mx_ref.flush((rng.standard_normal(shape, dtype=np.float32) * np.exp2(rng.integers(-2, 3, shape[:-1] + (1,)))).astype(BF))
    return {"a": f(N, 128, 4 * 512), "b": f(N, 128, KB * 4 * NC)}
def setup_inputs_blocks(rng):
    d = setup_inputs(rng)
    for k in ("a", "b"): d[k] = mx_ref.spread(d[k], rng, 2)
    return d
def setup_inputs_wide(rng):
    d = setup_inputs(rng)
    for k in ("a", "b"): d[k] = mx_ref.flush((d[k].astype(np.float32) * np.exp2(rng.integers(-4, 5, (N, 1, 1))).astype(np.float32)).astype(BF))
    return d
def setup_inputs_lossless(rng):
    a = np.zeros((N, 128, 4 * 128, 4), np.float32)
    for r in range(N):
        k = rng.integers(0, 512, size=4 * 128)
        a[r, k // 4, np.arange(4 * 128), k % 4] = 1.0
    size = np.repeat(2.0 ** rng.integers(-4, 5, size=(1, 1, (KB * 4 * NC) // 4)), 4, axis=2)
    b = rng.integers(-1, 2, size=(N, 128, KB * 4 * NC)) * size
    return {"a": a.reshape(N, 128, 4 * 512).astype(BF), "b": b.astype(np.float32).astype(BF)}
def reference(a, b):
    y = np.zeros((N, 128, KB * 4 * NC), np.float32)
    for k in range(KB):
        y[:, :, 4 * NC * k:4 * NC * k + 4 * NC] = mx_ref.total([term(a[r], mx_ref.quantize(cut(b[r], k, 4 * NC))) for r in range(N)])
    return {"y": y}

@@ -1,0 +1,244 @@
+from concourse.bass import DstId, RemoteDMATransfer
+from concourse.mybir import dt, AluOpType, ActivationFunctionType
+
+W = 128
+SLOTS = ["M0", "M1", "M2", "M3", "M4", "P1", "P2", "NEAR", "CAB", "FAR", "S"]
+SCRATCH = {
+    "at": ("sbuf", [128, 2048], "bfloat16"), "bt": ("sbuf", [128, 512], "bfloat16"),
+    "ones": ("sbuf", [128, 516], "bfloat16"), "diag": ("sbuf", [128, 516], "bfloat16"),
+    "h1": ("sbuf", [128, 512], "bfloat16"), "h2": ("sbuf", [128, 512], "bfloat16"),
+    "aq": ("sbuf", [128, 512], "float8_e4m3fn_x4"), "asc": ("sbuf", [128, 512], "uint8"),
+    "bq": ("sbuf", [128, 128], "float8_e4m3fn_x4"), "bsc": ("sbuf", [128, 128], "uint8"),
+    "eq": ("sbuf", [128, 512], "float8_e4m3fn_x4"), "esc": ("sbuf", [128, 512], "uint8"),
+    "q1": ("sbuf", [128, 128], "float8_e4m3fn_x4"), "p1": ("sbuf", [128, 128], "uint8"),
+    "q2": ("sbuf", [128, 128], "float8_e4m3fn_x4"), "p2": ("sbuf", [128, 128], "uint8"),
+    "yt": ("sbuf", [128, 512], "float32"),
+    "acc": ("psum", [128, 2048], "float32"), "tot": ("psum", [128, 2048], "float32"),
+}
+for _s in SLOTS:
+    SCRATCH["lq_" + _s] = ("sbuf", [128, 128], "float8_e4m3fn_x4")
+    SCRATCH["lp_" + _s] = ("sbuf", [128, 128], "uint8")
+SEMAPHORES = (["lb", "la", "la3", "one", "dg", "eqd", "bqd", "h1d", "t1", "h2d", "t2", "ycp", "yst", "sent"]
+              + ["aq%d" % i for i in range(4)] + ["pr%d" % i for i in range(4)] + ["su%d" % i for i in range(4)]
+              + ["yb%d" % i for i in range(4)] + ["c_" + s for s in SLOTS] + ["s_" + s for s in SLOTS])
+
+
+def roles(T, topo):
+    hosts = {}
+    for c in T.cores:
+        hosts.setdefault(topo.host(c), []).append(c)
+    team = max(hosts.values(), key=len)
+    hub = team[0]
+    near = cab = far = None
+    for c in T.cores:
+        if c in team:
+            continue
+        if not topo.may_write(hub, c):
+            far = c
+        elif topo.rack(topo.host(c)) == topo.rack(topo.host(hub)):
+            near = c
+        else:
+            cab = c
+    return team, near, cab, far
+
+
+def engines(topo, src, dsts, k):
+    m = -1
+    for d in dsts:
+        m &= topo.mask(src, d)
+    out, n = 0, 0
+    for e in range(m.bit_length()):
+        if m >> e & 1 and n < k:
+            out |= 1 << e
+            n += 1
+    return out, n
+
+
+def routes(T, topo):
+    team, near, cab, far = roles(T, topo)
+    hub = team[0]
+    R = []
+
+    def add(src, dsts, slot, parts, what, k):
+        for p in parts:
+            mask, n = engines(topo, src, dsts, k)
+            R.append((src, list(dsts), slot, p, what, mask, n))
+
+    others = lambda c: [d for d in team if d != c]
+    add(hub, team[1:], "M0", "cs", "1", 16)
+    for i in range(1, 5):
+        add(team[i], [hub], "M%d" % i, "cs", "1", 8)
+    add(team[3], [d for d in others(team[3]) if d != hub], "M3", "cs", "1", 16)
+    add(team[4], [d for d in others(team[4]) if d != hub], "M4", "cs", "1", 16)
+    add(hub, [near], "S", "c", "2", 8)
+    add(hub, [cab], "S", "s", "2", 8)
+    add(hub, [near], "S", "s", "2", 8)
+    add(hub, [cab], "S", "c", "2", 8)
+    add(near, [team[1]], "NEAR", "cs", "1", 8)
+    add(cab, [team[2]], "CAB", "cs", "1", 8)
+    add(far, [cab], "FAR", "c", "1", 8)
+    add(far, [near], "FAR", "s", "1", 8)
+    add(far, [near], "FAR", "c", "1", 8)
+    add(far, [cab], "FAR", "s", "1", 8)
+    add(near, [far], "NEAR", "cs", "1", 8)
+    add(cab, [far], "CAB", "cs", "1", 8)
+    add(cab, [team[3]], "FAR", "c", "FAR", 8)
+    add(near, [team[4]], "FAR", "s", "FAR", 8)
+    add(far, [cab], "NEAR", "cs", "NEAR", 8)
+    add(far, [near], "CAB", "cs", "CAB", 8)
+    add(team[1], others(team[1]), "P1", "cs", "2", 16)
+    add(team[2], others(team[2]), "P2", "cs", "2", 16)
+    add(team[3], others(team[3]), "FAR", "c", "FAR", 16)
+    add(team[4], others(team[4]), "FAR", "s", "FAR", 16)
+    add(near, [far], "S", "c", "S", 8)
+    add(cab, [far], "S", "s", "S", 8)
+    return R
+
+
+def rank_program(g, core, T, topo):
+    if T.rank_of(core) is None:
+        return
+    team, near, cab, far = roles(T, topo)
+    hub = team[0]
+    R = routes(T, topo)
+    S = T.sem
+    Copy = ActivationFunctionType.Copy
+
+    def need(slot, part):
+        return [r[6] for r in R if core in r[1] and r[2] == slot and r[3] == part][0]
+
+    if core == hub:
+        first, total = ["M1", "M2", "M3", "M4"], ["M3", "M4", "P1", "P2", "FAR"]
+    elif core == team[1]:
+        first, total = ["NEAR"], ["NEAR", "M3", "M4", "M0", "P2", "FAR"]
+    elif core == team[2]:
+        first, total = ["CAB"], ["CAB", "M3", "M4", "M0", "P1", "FAR"]
+    elif core == team[3]:
+        first, total = [], ["M4", "M0", "P1", "P2", "FAR"]
+    elif core == team[4]:
+        first, total = [], ["M3", "M0", "P1", "P2", "FAR"]
+    elif core == near:
+        first, total = [], ["FAR", "CAB", "S"]
+    elif core == cab:
+        first, total = [], ["FAR", "NEAR", "S"]
+    else:
+        first, total = [], ["NEAR", "CAB", "S"]
+
+    g.scalar.dma_start(T.at[:, 0:1536], T.a[:, 0:1536]).then_inc(S.la, 16)
+    g.sync.dma_start(T.bt[:], T.b[:]).then_inc(S.lb, 16)
+    g.sync.dma_start(T.at[:, 1536:2048], T.a[:, 1536:2048]).then_inc(S.la3, 16)
+
+    g.vector.memset(T.ones[:], 1.0).then_inc(S.one, 1)
+    g.wait_ge(S.one, 1)
+    g.affine_select(T.diag[:], T.ones[:], [[1, 516]], AluOpType.is_equal, 0.0, -3, -4).then_inc(S.dg, 1)
+    g.vector.wait_ge(S.dg, 1)
+    for b in range(4):
+        g.vector.quantize_mx(T.eq[:, W * b:W * b + W], T.esc[:, W * b:W * b + W], T.diag[:, 3 - b:515 - b]).then_inc(S.eqd, 1)
+    g.vector.wait_ge(S.lb, 16)
+    g.vector.quantize_mx(T.bq[:], T.bsc[:], T.bt[:]).then_inc(S.bqd, 1)
+    g.vector.wait_ge(S.la, 16)
+    for i in range(4):
+        if i == 3:
+            g.vector.wait_ge(S.la3, 16)
+        g.vector.quantize_mx(T.aq[:, W * i:W * i + W], T.asc[:, W * i:W * i + W],
+                             T.at[:, 512 * i:512 * i + 512]).then_inc(S["aq%d" % i], 1)
+
+    def product(bank, i, stop):
+        return g.tensor.matmul_mx(bank[:, 512 * i:512 * i + W], T.aq[:, W * i:W * i + W], T.asc[:, W * i:W * i + W],
+                                  T.bq[:], T.bsc[:], True, stop)
+
+    def unpack(bank, slot, b, stop):
+        return g.tensor.matmul_mx(bank[:, 512 * b:512 * b + W], T.eq[:, W * b:W * b + W], T.esc[:, W * b:W * b + W],
+                                  T["lq_" + slot][:], T["lp_" + slot][:], False, stop)
+
+    g.tensor.wait_ge(S.bqd, 1)
+    for i in range(4):
+        g.tensor.wait_ge(S["aq%d" % i], 1)
+        product(T.acc, i, True).then_inc(S["pr%d" % i], 1)
+    for i in range(4):
+        product(T.tot, i, False)
+    g.tensor.wait_ge(S.eqd, 4)
+    waited = []
+
+    def arrive(slot):
+        if slot not in waited:
+            waited.append(slot)
+            g.tensor.wait_ge(S["c_" + slot], need(slot, "c"))
+            g.tensor.wait_ge(S["s_" + slot], need(slot, "s"))
+
+    if first:
+        g.tensor.wait_ge(S.h1d, 4)
+        for i in range(4):
+            product(T.acc, i, False)
+        for slot in first:
+            arrive(slot)
+            for b in range(4):
+                last = slot == first[-1]
+                u = unpack(T.acc, slot, b, last)
+                if last:
+                    u.then_inc(S["su%d" % b], 1)
+    for slot in total:
+        arrive(slot)
+        for b in range(4):
+            last = slot == total[-1]
+            u = unpack(T.tot, slot, b, last)
+            if last:
+                u.then_inc(S["yb%d" % b], 1)
+
+    for b in range(3):
+        g.scalar.wait_ge(S["pr%d" % b], 1)
+        g.scalar.activation(T.h1[:, b:512:4], T.acc[:, 512 * b:512 * b + W], Copy).then_inc(S.h1d, 1)
+    g.vector.wait_ge(S.pr3, 1)
+    g.vector.tensor_copy(T.h1[:, 3:512:4], T.acc[:, 1536:1536 + W]).then_inc(S.h1d, 1)
+    g.vector.wait_ge(S.h1d, 4)
+    g.vector.quantize_mx(T.q1[:], T.p1[:], T.h1[:]).then_inc(S.t1, 1)
+
+    def evict(out, bank, ready, done):
+        for b in range(4):
+            src, dst = bank[:, 512 * b:512 * b + W], out[:, b:512:4]
+            if b % 2 == 0:
+                g.scalar.wait_ge(S["%s%d" % (ready, b)], 1)
+                g.scalar.activation(dst, src, Copy).then_inc(S[done], 1)
+            else:
+                g.vector.wait_ge(S["%s%d" % (ready, b)], 1)
+                g.vector.tensor_copy(dst, src).then_inc(S[done], 1)
+
+    if first:
+        evict(T.h2, T.acc, "su", "h2d")
+        g.vector.wait_ge(S.h2d, 4)
+        g.vector.quantize_mx(T.q2[:], T.p2[:], T.h2[:]).then_inc(S.t2, 1)
+    evict(T.yt, T.tot, "yb", "ycp")
+    g.sync.wait_ge(S.ycp, 4)
+    g.sync.dma_start(T.y[:], T.yt[:]).then_inc(S.yst, 16)
+    g.sync.wait_ge(S.yst, 16)
+
+    seen, sent = [], 0
+    for src, dsts, slot, part, what, mask, n in R:
+        if src != core:
+            continue
+        if what in ("1", "2"):
+            key, sem, val = what, S["t" + what], 1
+            q, p = T["q" + what], T["p" + what]
+        else:
+            key, sem, val = what + part, S[part + "_" + what], need(what, part)
+            q, p = T["lq_" + what], T["lp_" + what]
+        if key not in seen:
+            seen.append(key)
+            g.wait_ge(sem, val)
+        if part == "c":
+            ap_in, ap_out = q[:].bitcast(dt.uint8), T["lq_" + slot][:].bitcast(dt.uint8)
+        else:
+            ap_in, ap_out = p[:], T["lp_" + slot][:]
+        if len(dsts) == 1:
+            rid, pid = topo.addr(dsts[0], core)
+            g.remote_dma(out_ap=ap_out, in_ap=ap_in, remote_sem=S[part + "_" + slot], local_sem=S.sent, pid=pid,
+                         routing_id=rid, dma_engine_mask=mask)
+        else:
+            ids = []
+            for d in dsts:
+                rid, pid = topo.addr(d, core)
+                ids.append(DstId(rid=rid, pnc=pid))
+            g.remote_dma_fused([RemoteDMATransfer(dst_ids=ids, dma_engine_mask=mask, remote_sem=S[part + "_" + slot],
+                                                  srcs=[ap_in], dsts=[ap_out for _ in dsts], alu_op=0)], local_sem=S.sent)
+        sent += n
+    g.wait_ge(S.sent, sent)

@@ -2,25 +2,33 @@ from concourse.bass import DstId, RemoteDMATransfer
 from concourse.mybir import dt, AluOpType, ActivationFunctionType
 
 W = 128
-SLOTS = ["M0", "M1", "M2", "M3", "M4", "P1", "P2", "NEAR", "CAB", "FAR", "S"]
+H = 64
+SLOTS = ["M0", "M1", "M2", "M3", "M4", "NEAR", "CAB", "FAR"]
+HUBS = [0, 2]
+TO = {0: 1, 1: 4, 4: 0, 2: 3, 3: 2}
+GIVES = {0: 0, 1: 1, 4: 2, 2: 0, 3: 1}
 SCRATCH = {
     "at": ("sbuf", [128, 2048], "bfloat16"), "bt": ("sbuf", [128, 512], "bfloat16"),
     "ones": ("sbuf", [128, 516], "bfloat16"), "diag": ("sbuf", [128, 516], "bfloat16"),
+    "ft": ("sbuf", [128, 1024], "bfloat16"),
     "h1": ("sbuf", [128, 512], "bfloat16"), "h2": ("sbuf", [128, 512], "bfloat16"),
     "aq": ("sbuf", [128, 512], "float8_e4m3fn_x4"), "asc": ("sbuf", [128, 512], "uint8"),
     "bq": ("sbuf", [128, 128], "float8_e4m3fn_x4"), "bsc": ("sbuf", [128, 128], "uint8"),
     "eq": ("sbuf", [128, 512], "float8_e4m3fn_x4"), "esc": ("sbuf", [128, 512], "uint8"),
+    "fq": ("sbuf", [128, 256], "float8_e4m3fn_x4"), "fsc": ("sbuf", [128, 256], "uint8"),
     "q1": ("sbuf", [128, 128], "float8_e4m3fn_x4"), "p1": ("sbuf", [128, 128], "uint8"),
     "q2": ("sbuf", [128, 128], "float8_e4m3fn_x4"), "p2": ("sbuf", [128, 128], "uint8"),
+    "lq_S": ("sbuf", [128, 128], "float8_e4m3fn_x4"), "lp_S": ("sbuf", [128, 128], "uint8"),
     "yt": ("sbuf", [128, 512], "float32"),
     "acc": ("psum", [128, 2048], "float32"), "tot": ("psum", [128, 2048], "float32"),
 }
 for _s in SLOTS:
     SCRATCH["lq_" + _s] = ("sbuf", [128, 128], "float8_e4m3fn_x4")
     SCRATCH["lp_" + _s] = ("sbuf", [128, 128], "uint8")
-SEMAPHORES = (["lb", "la", "la3", "one", "dg", "eqd", "bqd", "h1d", "t1", "h2d", "t2", "ycp", "yst", "sent"]
-              + ["aq%d" % i for i in range(4)] + ["pr%d" % i for i in range(4)] + ["su%d" % i for i in range(4)]
-              + ["yb%d" % i for i in range(4)] + ["c_" + s for s in SLOTS] + ["s_" + s for s in SLOTS])
+SEMAPHORES = (["lb", "la", "la3", "one", "dg", "eqd", "egd", "ftd", "fqd", "bqd", "h1d", "t1", "h2z", "h2d", "t2", "ycp", "yst", "sent",
+               "su0", "su1"]
+              + ["aq%d" % i for i in range(4)] + ["pr%d" % i for i in range(4)] + ["yb%d" % i for i in range(4)]
+              + [p + s for p in ("c_", "s_") for s in SLOTS + ["S0", "S1", "E0", "E1", "E2", "E3"]])
 
 
 def roles(T, topo):
@@ -28,14 +36,13 @@ def roles(T, topo):
     for c in T.cores:
         hosts.setdefault(topo.host(c), []).append(c)
     team = max(hosts.values(), key=len)
-    hub = team[0]
     near = cab = far = None
     for c in T.cores:
         if c in team:
             continue
-        if not topo.may_write(hub, c):
+        if not topo.may_write(team[0], c):
             far = c
-        elif topo.rack(topo.host(c)) == topo.rack(topo.host(hub)):
+        elif topo.rack(topo.host(c)) == topo.rack(topo.host(team[0])):
             near = c
         else:
             cab = c
@@ -46,17 +53,15 @@ def engines(topo, src, dsts, k):
     m = -1
     for d in dsts:
         m &= topo.mask(src, d)
-    out, n = 0, 0
-    for e in range(m.bit_length()):
-        if m >> e & 1 and n < k:
-            out |= 1 << e
-            n += 1
-    return out, n
+    es = [e for e in range(m.bit_length()) if m >> e & 1]
+    es = es[:k] if k > 0 else es[k:]
+    return sum(1 << e for e in es), len(es)
 
 
 def routes(T, topo):
     team, near, cab, far = roles(T, topo)
-    hub = team[0]
+    hubs = [team[i] for i in HUBS]
+    t1, t3, t4 = [c for c in team if c not in hubs]
     R = []
 
     def add(src, dsts, slot, parts, what, k):
@@ -64,34 +69,38 @@ def routes(T, topo):
             mask, n = engines(topo, src, dsts, k)
             R.append((src, list(dsts), slot, p, what, mask, n))
 
-    others = lambda c: [d for d in team if d != c]
-    add(hub, team[1:], "M0", "cs", "1", 16)
-    for i in range(1, 5):
-        add(team[i], [hub], "M%d" % i, "cs", "1", 8)
-    add(team[3], [d for d in others(team[3]) if d != hub], "M3", "cs", "1", 16)
-    add(team[4], [d for d in others(team[4]) if d != hub], "M4", "cs", "1", 16)
-    add(hub, [near], "S", "c", "2", 8)
-    add(hub, [cab], "S", "s", "2", 8)
-    add(hub, [near], "S", "s", "2", 8)
-    add(hub, [cab], "S", "c", "2", 8)
-    add(near, [team[1]], "NEAR", "cs", "1", 8)
-    add(cab, [team[2]], "CAB", "cs", "1", 8)
+    def others(m, cores):
+        return [d for d in cores if d != m]
+
+    for i in range(5):
+        add(team[i], [team[TO[i]]], "E%d" % GIVES[i], "cs", "E", 16)
+    for i in range(5):
+        add(team[i], others(team[i], hubs), "M%d" % i, "cs", "1", 16)
+        add(team[i], others(team[i], [t1, t3, t4]), "M%d" % i, "cs", "1", 16)
+    add(hubs[0], [near], "S0", "cs", "2", 8)
+    add(hubs[1], [cab], "S1", "cs", "2", 8)
+    add(near, [t1], "NEAR", "c", "1", 8)
+    add(near, [t4], "NEAR", "s", "1", 8)
+    add(cab, [t3], "CAB", "c", "1", 8)
+    add(cab, [hubs[0]], "CAB", "s", "1", 8)
     add(far, [cab], "FAR", "c", "1", 8)
     add(far, [near], "FAR", "s", "1", 8)
     add(far, [near], "FAR", "c", "1", 8)
     add(far, [cab], "FAR", "s", "1", 8)
+    add(cab, [t1], "FAR", "c", "FAR", 8)
+    add(near, [t3], "FAR", "s", "FAR", 8)
     add(near, [far], "NEAR", "cs", "1", 8)
     add(cab, [far], "CAB", "cs", "1", 8)
-    add(cab, [team[3]], "FAR", "c", "FAR", 8)
-    add(near, [team[4]], "FAR", "s", "FAR", 8)
-    add(far, [cab], "NEAR", "cs", "NEAR", 8)
-    add(far, [near], "CAB", "cs", "CAB", 8)
-    add(team[1], others(team[1]), "P1", "cs", "2", 16)
-    add(team[2], others(team[2]), "P2", "cs", "2", 16)
-    add(team[3], others(team[3]), "FAR", "c", "FAR", 16)
-    add(team[4], others(team[4]), "FAR", "s", "FAR", 16)
-    add(near, [far], "S", "c", "S", 8)
-    add(cab, [far], "S", "s", "S", 8)
+    for m, away, slot, part, k in ((t1, cab, "NEAR", "c", 16), (t3, near, "CAB", "c", 16), (t4, cab, "NEAR", "s", 16),
+                                   (hubs[0], near, "CAB", "s", -8)):
+        add(m, others(m, team), slot, part, slot, k)
+        add(m, [away], slot, part, slot, 8)
+    add(t1, others(t1, team), "FAR", "c", "FAR", 16)
+    add(t3, others(t3, team), "FAR", "s", "FAR", 16)
+    add(hubs[0], [cab], "S0", "cs", "2", 8)
+    add(hubs[1], [near], "S1", "cs", "2", 8)
+    add(near, [far], "S0", "cs", "S0", 8)
+    add(cab, [far], "S1", "cs", "S1", 8)
     return R
 
 
@@ -99,7 +108,10 @@ def rank_program(g, core, T, topo):
     if T.rank_of(core) is None:
         return
     team, near, cab, far = roles(T, topo)
-    hub = team[0]
+    half = None
+    for k, i in enumerate(HUBS):
+        if team[i] == core:
+            half = k
     R = routes(T, topo)
     S = T.sem
     Copy = ActivationFunctionType.Copy
@@ -107,22 +119,18 @@ def rank_program(g, core, T, topo):
     def need(slot, part):
         return [r[6] for r in R if core in r[1] and r[2] == slot and r[3] == part][0]
 
-    if core == hub:
-        first, total = ["M1", "M2", "M3", "M4"], ["M3", "M4", "P1", "P2", "FAR"]
-    elif core == team[1]:
-        first, total = ["NEAR"], ["NEAR", "M3", "M4", "M0", "P2", "FAR"]
-    elif core == team[2]:
-        first, total = ["CAB"], ["CAB", "M3", "M4", "M0", "P1", "FAR"]
-    elif core == team[3]:
-        first, total = [], ["M4", "M0", "P1", "P2", "FAR"]
-    elif core == team[4]:
-        first, total = [], ["M3", "M0", "P1", "P2", "FAR"]
-    elif core == near:
-        first, total = [], ["FAR", "CAB", "S"]
-    elif core == cab:
-        first, total = [], ["FAR", "NEAR", "S"]
+    mates = ["M%d" % i for i in (1, 3, 4, 0, 2) if team[i] != core]
+    if core in team:
+        total = mates + ["NEAR", "CAB", "FAR"]
     else:
-        first, total = [], ["NEAR", "CAB", "S"]
+        total = [s for s, own in (("FAR", far), ("NEAR", near), ("CAB", cab)) if own != core] + ["S"]
+
+    gets = [r[2] for r in R if core in r[1] and r[4] == "E" and r[3] == "c"]
+    makes = [b for b in range(4) if "E%d" % b not in gets]
+    give = None
+    if core in team:
+        give = GIVES[team.index(core)]
+        makes.remove(give)
 
     g.scalar.dma_start(T.at[:, 0:1536], T.a[:, 0:1536]).then_inc(S.la, 16)
     g.sync.dma_start(T.bt[:], T.b[:]).then_inc(S.lb, 16)
@@ -131,9 +139,24 @@ def rank_program(g, core, T, topo):
     g.vector.memset(T.ones[:], 1.0).then_inc(S.one, 1)
     g.wait_ge(S.one, 1)
     g.affine_select(T.diag[:], T.ones[:], [[1, 516]], AluOpType.is_equal, 0.0, -3, -4).then_inc(S.dg, 1)
+    if half is not None:
+        g.scalar.wait_ge(S.dg, 1)
+        for b in range(4):
+            at = 3 - b + 4 * H * half
+            g.scalar.activation(T.ft[:, 4 * H * b:4 * H * b + 4 * H], T.diag[:, at:at + 4 * H], Copy).then_inc(S.ftd, 1)
+        g.vector.memset(T.h2[:, 4 * H:512], 0.0).then_inc(S.h2z, 1)
     g.vector.wait_ge(S.dg, 1)
-    for b in range(4):
-        g.vector.quantize_mx(T.eq[:, W * b:W * b + W], T.esc[:, W * b:W * b + W], T.diag[:, 3 - b:515 - b]).then_inc(S.eqd, 1)
+
+    def select(b):
+        return g.vector.quantize_mx(T.eq[:, W * b:W * b + W], T.esc[:, W * b:W * b + W], T.diag[:, 3 - b:515 - b])
+
+    if give is not None:
+        select(give).then_inc(S.egd, 1)
+    for b in makes:
+        select(b).then_inc(S.eqd, 1)
+    if half is not None:
+        g.vector.wait_ge(S.ftd, 4)
+        g.vector.quantize_mx(T.fq[:], T.fsc[:], T.ft[:]).then_inc(S.fqd, 1)
     g.vector.wait_ge(S.lb, 16)
     g.vector.quantize_mx(T.bq[:], T.bsc[:], T.bt[:]).then_inc(S.bqd, 1)
     g.vector.wait_ge(S.la, 16)
@@ -143,46 +166,51 @@ def rank_program(g, core, T, topo):
         g.vector.quantize_mx(T.aq[:, W * i:W * i + W], T.asc[:, W * i:W * i + W],
                              T.at[:, 512 * i:512 * i + 512]).then_inc(S["aq%d" % i], 1)
 
-    def product(bank, i, stop):
+    def product(bank, i, start, stop):
         return g.tensor.matmul_mx(bank[:, 512 * i:512 * i + W], T.aq[:, W * i:W * i + W], T.asc[:, W * i:W * i + W],
-                                  T.bq[:], T.bsc[:], True, stop)
+                                  T.bq[:], T.bsc[:], start, stop)
 
-    def unpack(bank, slot, b, stop):
-        return g.tensor.matmul_mx(bank[:, 512 * b:512 * b + W], T.eq[:, W * b:W * b + W], T.esc[:, W * b:W * b + W],
-                                  T["lq_" + slot][:], T["lp_" + slot][:], False, stop)
+    def arrive(slot):
+        for s in (["S0", "S1"] if slot == "S" else [slot]):
+            g.tensor.wait_ge(S["c_" + s], need(s, "c"))
+            g.tensor.wait_ge(S["s_" + s], need(s, "s"))
 
     g.tensor.wait_ge(S.bqd, 1)
     for i in range(4):
         g.tensor.wait_ge(S["aq%d" % i], 1)
-        product(T.acc, i, True).then_inc(S["pr%d" % i], 1)
+        product(T.acc, i, True, True).then_inc(S["pr%d" % i], 1)
     for i in range(4):
-        product(T.tot, i, False)
-    g.tensor.wait_ge(S.eqd, 4)
-    waited = []
-
-    def arrive(slot):
-        if slot not in waited:
-            waited.append(slot)
-            g.tensor.wait_ge(S["c_" + slot], need(slot, "c"))
-            g.tensor.wait_ge(S["s_" + slot], need(slot, "s"))
-
-    if first:
-        g.tensor.wait_ge(S.h1d, 4)
-        for i in range(4):
-            product(T.acc, i, False)
-        for slot in first:
-            arrive(slot)
-            for b in range(4):
-                last = slot == first[-1]
-                u = unpack(T.acc, slot, b, last)
-                if last:
-                    u.then_inc(S["su%d" % b], 1)
-    for slot in total:
+        product(T.tot, i, True, False)
+    if half is not None:
+        g.tensor.wait_ge(S.fqd, 1)
+        g.tensor.wait_ge(S.t1, 1)
+        for slot in ["OWN"] + mates:
+            if slot != "OWN":
+                arrive(slot)
+            q, p = (T.q1, T.p1) if slot == "OWN" else (T["lq_" + slot], T["lp_" + slot])
+            for k in range(2):
+                u = g.tensor.matmul_mx(T.acc[:, 512 * k:512 * k + W], q[:], p[:], T.fq[:, W * k:W * k + W], T.fsc[:, W * k:W * k + W],
+                                       slot == "OWN", slot == mates[-1])
+                if slot == mates[-1]:
+                    u.then_inc(S["su%d" % k], 1)
+    g.tensor.wait_ge(S.eqd, len(makes))
+    if give is not None:
+        g.tensor.wait_ge(S.egd, 1)
+    for slot in gets:
         arrive(slot)
+    for slot in total:
+        if half is None or slot not in mates:
+            arrive(slot)
+        q, p = ("lq_" + slot), ("lp_" + slot)
+        q, p = T[q][:], T[p][:]
         for b in range(4):
-            last = slot == total[-1]
-            u = unpack(T.tot, slot, b, last)
-            if last:
+            out = T.tot[:, 512 * b:512 * b + W]
+            e, x = T.eq[:, W * b:W * b + W], T.esc[:, W * b:W * b + W]
+            if slot == "S":
+                u = g.tensor.matmul_mx(out, q, p, e, x, False, slot == total[-1])
+            else:
+                u = g.tensor.matmul_mx(out, e, x, q, p, False, slot == total[-1])
+            if slot == total[-1]:
                 u.then_inc(S["yb%d" % b], 1)
 
     for b in range(3):
@@ -193,21 +221,25 @@ def rank_program(g, core, T, topo):
     g.vector.wait_ge(S.h1d, 4)
     g.vector.quantize_mx(T.q1[:], T.p1[:], T.h1[:]).then_inc(S.t1, 1)
 
-    def evict(out, bank, ready, done):
-        for b in range(4):
-            src, dst = bank[:, 512 * b:512 * b + W], out[:, b:512:4]
-            if b % 2 == 0:
-                g.scalar.wait_ge(S["%s%d" % (ready, b)], 1)
-                g.scalar.activation(dst, src, Copy).then_inc(S[done], 1)
-            else:
-                g.vector.wait_ge(S["%s%d" % (ready, b)], 1)
-                g.vector.tensor_copy(dst, src).then_inc(S[done], 1)
-
-    if first:
-        evict(T.h2, T.acc, "su", "h2d")
+    if half is not None:
+        g.scalar.wait_ge(S.su0, 1)
+        for b in (0, 1):
+            g.scalar.activation(T.h2[:, b:4 * H:4], T.acc[:, H * b:H * b + H], Copy).then_inc(S.h2d, 1)
+        g.vector.wait_ge(S.su1, 1)
+        for b in (2, 3):
+            g.vector.tensor_copy(T.h2[:, b:4 * H:4], T.acc[:, 512 + H * (b - 2):512 + H * (b - 2) + H]).then_inc(S.h2d, 1)
+        g.vector.wait_ge(S.h2z, 1)
         g.vector.wait_ge(S.h2d, 4)
         g.vector.quantize_mx(T.q2[:], T.p2[:], T.h2[:]).then_inc(S.t2, 1)
-    evict(T.yt, T.tot, "yb", "ycp")
+
+    for b in range(4):
+        src, dst = T.tot[:, 512 * b:512 * b + W], T.yt[:, b:512:4]
+        if b % 2 == 0:
+            g.scalar.wait_ge(S["yb%d" % b], 1)
+            g.scalar.activation(dst, src, Copy).then_inc(S.ycp, 1)
+        else:
+            g.vector.wait_ge(S["yb%d" % b], 1)
+            g.vector.tensor_copy(dst, src).then_inc(S.ycp, 1)
     g.sync.wait_ge(S.ycp, 4)
     g.sync.dma_start(T.y[:], T.yt[:]).then_inc(S.yst, 16)
     g.sync.wait_ge(S.yst, 16)
@@ -216,19 +248,29 @@ def rank_program(g, core, T, topo):
     for src, dsts, slot, part, what, mask, n in R:
         if src != core:
             continue
-        if what in ("1", "2"):
-            key, sem, val = what, S["t" + what], 1
-            q, p = T["q" + what], T["p" + what]
+        lo, hi, ql, pl = 0, W, "lq_" + slot, "lp_" + slot
+        if slot[0] == "S":
+            lo = H * int(slot[1])
+            hi, ql, pl = lo + H, "lq_S", "lp_S"
+        if what == "E":
+            key, sem, val = what, S.egd, 1
+            q, p = T.eq[:, W * give:W * give + W], T.esc[:, W * give:W * give + W]
+            q_out, p_out = q, p
         else:
-            key, sem, val = what + part, S[part + "_" + what], need(what, part)
-            q, p = T["lq_" + what], T["lp_" + what]
+            q_out, p_out = T[ql][:, lo:hi], T[pl][:, lo:hi]
+            if what in ("1", "2"):
+                key, sem, val = what, S["t" + what], 1
+                q, p = T["q" + what][:, 0:hi - lo], T["p" + what][:, 0:hi - lo]
+            else:
+                key, sem, val = what + part, S[part + "_" + what], need(what, part)
+                q, p = q_out, p_out
         if key not in seen:
             seen.append(key)
             g.wait_ge(sem, val)
         if part == "c":
-            ap_in, ap_out = q[:].bitcast(dt.uint8), T["lq_" + slot][:].bitcast(dt.uint8)
+            ap_in, ap_out = q.bitcast(dt.uint8), q_out.bitcast(dt.uint8)
         else:
-            ap_in, ap_out = p[:], T["lp_" + slot][:]
+            ap_in, ap_out = p, p_out
         if len(dsts) == 1:
             rid, pid = topo.addr(dsts[0], core)
             g.remote_dma(out_ap=ap_out, in_ap=ap_in, remote_sem=S[part + "_" + slot], local_sem=S.sent, pid=pid,

@@ -3,28 +3,23 @@ from concourse.mybir import dt, AluOpType, ActivationFunctionType
 
 W = 128
 H = 64
+WORLD = 512
 SLOTS = ["M0", "M1", "M2", "M3", "M4", "NEAR", "CAB", "FAR"]
 HUBS = [0, 2]
+SENDS = {0: [2, 1, 3, 4], 2: [0, 3, 4, 1], 1: [0, 2, 4, 3], 4: [0, 2, 3, 1], 3: [2, 0, 1, 4]}
+LAND = {"NEARc": 1, "NEARs": 4, "CABc": 7, "CABs": 3, "FARc": 3, "FARs": 4}
+AWAY_FIRST = ("CABc", "CABs", "NEARs")
 TO = {0: 1, 1: 4, 4: 0, 2: 3, 3: 2}
 GIVES = {0: 0, 1: 1, 4: 2, 2: 0, 3: 1}
-SCRATCH = {
-    "at": ("sbuf", [128, 2048], "bfloat16"), "bt": ("sbuf", [128, 512], "bfloat16"),
-    "ones": ("sbuf", [128, 516], "bfloat16"), "diag": ("sbuf", [128, 516], "bfloat16"),
-    "ft": ("sbuf", [128, 1024], "bfloat16"),
-    "h1": ("sbuf", [128, 512], "bfloat16"), "h2": ("sbuf", [128, 512], "bfloat16"),
-    "aq": ("sbuf", [128, 512], "float8_e4m3fn_x4"), "asc": ("sbuf", [128, 512], "uint8"),
-    "bq": ("sbuf", [128, 128], "float8_e4m3fn_x4"), "bsc": ("sbuf", [128, 128], "uint8"),
-    "eq": ("sbuf", [128, 512], "float8_e4m3fn_x4"), "esc": ("sbuf", [128, 512], "uint8"),
-    "fq": ("sbuf", [128, 256], "float8_e4m3fn_x4"), "fsc": ("sbuf", [128, 256], "uint8"),
-    "q1": ("sbuf", [128, 128], "float8_e4m3fn_x4"), "p1": ("sbuf", [128, 128], "uint8"),
-    "q2": ("sbuf", [128, 128], "float8_e4m3fn_x4"), "p2": ("sbuf", [128, 128], "uint8"),
-    "lq_S": ("sbuf", [128, 128], "float8_e4m3fn_x4"), "lp_S": ("sbuf", [128, 128], "uint8"),
-    "yt": ("sbuf", [128, 512], "float32"),
-    "acc": ("psum", [128, 2048], "float32"), "tot": ("psum", [128, 2048], "float32"),
-}
-for _s in SLOTS:
-    SCRATCH["lq_" + _s] = ("sbuf", [128, 128], "float8_e4m3fn_x4")
-    SCRATCH["lp_" + _s] = ("sbuf", [128, 128], "uint8")
+BF, F8, U8 = "bfloat16", "float8_e4m3fn_x4", "uint8"
+SCRATCH = {"acc": ("psum", [128, 2048], "float32"), "tot": ("psum", [128, 2048], "float32"), "yt": ("sbuf", [128, 512], "float32")}
+for _n, _w, _d in (("at", 2048, BF), ("bt", 512, BF), ("ones", 516, BF), ("diag", 516, BF), ("ft", 1024, BF), ("h1", 512, BF), ("h2", 512, BF),
+                   ("aq", 512, F8), ("asc", 512, U8), ("bq", 128, F8), ("bsc", 128, U8), ("eq", 512, F8), ("esc", 512, U8),
+                   ("fq", 256, F8), ("fsc", 256, U8), ("q1", 128, F8), ("p1", 128, U8), ("q2", 128, F8), ("p2", 128, U8)):
+    SCRATCH[_n] = ("sbuf", [128, _w], _d)
+for _s in SLOTS + ["S"]:
+    SCRATCH["lq_" + _s] = ("sbuf", [128, 128], F8)
+    SCRATCH["lp_" + _s] = ("sbuf", [128, 128], U8)
 SEMAPHORES = (["lb", "la", "la3", "one", "dg", "eqd", "egd", "ftd", "fqd", "bqd", "h1d", "t1", "h2z", "h2d", "t2", "ycp", "yst", "sent",
                "su0", "su1"]
               + ["aq%d" % i for i in range(4)] + ["pr%d" % i for i in range(4)] + ["yb%d" % i for i in range(4)]
@@ -49,6 +44,13 @@ def roles(T, topo):
     return team, near, cab, far
 
 
+def helpers(T, topo, team, near, cab):
+    def free(x):
+        return [c for c in range(WORLD) if topo.host(c) == topo.host(x) and topo.chip(c) == topo.chip(x) and T.rank_of(c) is None]
+    return (free(team[0]), [c for c in free(near) if topo.die(c) != topo.die(near)][0],
+            [c for c in free(cab) if topo.die(c) != topo.die(cab)][0])
+
+
 def engines(topo, src, dsts, k):
     m = -1
     for d in dsts:
@@ -60,8 +62,10 @@ def engines(topo, src, dsts, k):
 
 def routes(T, topo):
     team, near, cab, far = roles(T, topo)
+    extra, nh, ch = helpers(T, topo, team, near, cab)
     hubs = [team[i] for i in HUBS]
-    t1, t3, t4 = [c for c in team if c not in hubs]
+    rest = [c for c in team if c not in hubs]
+    at = {k: (team + extra)[v] for k, v in LAND.items()}
     R = []
 
     def add(src, dsts, slot, parts, what, k):
@@ -69,102 +73,113 @@ def routes(T, topo):
             mask, n = engines(topo, src, dsts, k)
             R.append((src, list(dsts), slot, p, what, mask, n))
 
-    def others(m, cores):
-        return [d for d in cores if d != m]
-
+    add(extra[0], hubs, "E3", "cs", "E", 16)
+    add(extra[1], rest[:1], "E3", "cs", "E", 16)
+    add(extra[2], rest[1:], "E3", "cs", "E", 16)
+    add(nh, [near], "E3", "cs", "E", 16)
+    add(ch, [cab], "E3", "cs", "E", 16)
     for i in range(5):
         add(team[i], [team[TO[i]]], "E%d" % GIVES[i], "cs", "E", 16)
     for i in range(5):
-        add(team[i], others(team[i], hubs), "M%d" % i, "cs", "1", 16)
-        add(team[i], others(team[i], [t1, t3, t4]), "M%d" % i, "cs", "1", 16)
-    add(hubs[0], [near], "S0", "cs", "2", 8)
-    add(hubs[1], [cab], "S1", "cs", "2", 8)
-    add(near, [t1], "NEAR", "c", "1", 8)
-    add(near, [t4], "NEAR", "s", "1", 8)
-    add(cab, [t3], "CAB", "c", "1", 8)
-    add(cab, [hubs[0]], "CAB", "s", "1", 8)
-    add(far, [cab], "FAR", "c", "1", 8)
-    add(far, [near], "FAR", "s", "1", 8)
+        for d in SENDS[i]:
+            add(team[i], [team[d]], "M%d" % i, "cs", "1", 16)
+    for h, first, then, slot in ((hubs[0], near, cab, "S0"), (hubs[1], cab, near, "S1")):
+        add(h, [first], slot, "cs", "2", 8)
+        add(h, [then], slot, "cs", "2", 8)
+    for m, slot in ((near, "NEAR"), (cab, "CAB")):
+        add(m, [at[slot + "c"]], slot, "c", "1", 8)
+        add(m, [at[slot + "s"]], slot, "s", "1", 8)
+        add(m, [far], slot, "cs", "1", 8)
+    add(far, [ch], "FAR", "c", "1", 8)
+    add(far, [nh], "FAR", "s", "1", 8)
     add(far, [near], "FAR", "c", "1", 8)
     add(far, [cab], "FAR", "s", "1", 8)
-    add(cab, [t1], "FAR", "c", "FAR", 8)
-    add(near, [t3], "FAR", "s", "FAR", 8)
-    add(near, [far], "NEAR", "cs", "1", 8)
-    add(cab, [far], "CAB", "cs", "1", 8)
-    for m, away, slot, part, k in ((t1, cab, "NEAR", "c", 16), (t3, near, "CAB", "c", 16), (t4, cab, "NEAR", "s", 16),
-                                   (hubs[0], near, "CAB", "s", -8)):
-        add(m, others(m, team), slot, part, slot, k)
-        add(m, [away], slot, part, slot, 8)
-    add(t1, others(t1, team), "FAR", "c", "FAR", 16)
-    add(t3, others(t3, team), "FAR", "s", "FAR", 16)
-    add(hubs[0], [cab], "S0", "cs", "2", 8)
-    add(hubs[1], [near], "S1", "cs", "2", 8)
+    for m, lone, part in ((ch, cab, "c"), (nh, near, "s")):
+        add(m, [at["FAR" + part]], "FAR", part, "FAR", 8)
+        add(m, [lone], "FAR", part, "FAR", -8)
     add(near, [far], "S0", "cs", "S0", 8)
     add(cab, [far], "S1", "cs", "S1", 8)
+    for slot, part, away in (("NEAR", "c", cab), ("CAB", "c", near), ("NEAR", "s", cab), ("CAB", "s", near),
+                             ("FAR", "c", None), ("FAR", "s", None)):
+        m = at[slot + part]
+        if slot + part in AWAY_FIRST:
+            add(m, [away], slot, part, slot, 8)
+        for same in (False, True):
+            ds = [d for d in team if d != m and (topo.die(d) == topo.die(m)) == same]
+            if ds:
+                add(m, ds, slot, part, slot, 16)
+        if away is not None and slot + part not in AWAY_FIRST:
+            add(m, [away], slot, part, slot, 8)
     return R
 
 
 def rank_program(g, core, T, topo):
-    if T.rank_of(core) is None:
+    rank = T.rank_of(core) is not None
+    if not any(topo.host(c) == topo.host(core) and topo.chip(c) == topo.chip(core) for c in T.cores):
         return
     team, near, cab, far = roles(T, topo)
+    R = routes(T, topo)
+    if not any(core == r[0] or core in r[1] for r in R):
+        return
     half = None
     for k, i in enumerate(HUBS):
         if team[i] == core:
             half = k
-    R = routes(T, topo)
     S = T.sem
     Copy = ActivationFunctionType.Copy
 
     def need(slot, part):
         return [r[6] for r in R if core in r[1] and r[2] == slot and r[3] == part][0]
 
-    mates = ["M%d" % i for i in (1, 3, 4, 0, 2) if team[i] != core]
+    mates, total = [], []
     if core in team:
+        me = team.index(core)
+        mates = ["M%d" % i for _, i in sorted([(SENDS[i].index(me), i) for i in SENDS if i != me])]
         total = mates + ["NEAR", "CAB", "FAR"]
-    else:
+    elif rank:
         total = [s for s, own in (("FAR", far), ("NEAR", near), ("CAB", cab)) if own != core] + ["S"]
 
     gets = [r[2] for r in R if core in r[1] and r[4] == "E" and r[3] == "c"]
-    makes = [b for b in range(4) if "E%d" % b not in gets]
+    makes = [b for b in range(4) if "E%d" % b not in gets] if rank else []
     give = None
-    if core in team:
-        give = GIVES[team.index(core)]
+    for r in R:
+        if r[0] == core and r[4] == "E":
+            give = int(r[2][1])
+    if give in makes:
         makes.remove(give)
 
-    g.scalar.dma_start(T.at[:, 0:1536], T.a[:, 0:1536]).then_inc(S.la, 16)
-    g.sync.dma_start(T.bt[:], T.b[:]).then_inc(S.lb, 16)
-    g.sync.dma_start(T.at[:, 1536:2048], T.a[:, 1536:2048]).then_inc(S.la3, 16)
-
-    g.vector.memset(T.ones[:], 1.0).then_inc(S.one, 1)
-    g.wait_ge(S.one, 1)
-    g.affine_select(T.diag[:], T.ones[:], [[1, 516]], AluOpType.is_equal, 0.0, -3, -4).then_inc(S.dg, 1)
-    if half is not None:
-        g.scalar.wait_ge(S.dg, 1)
-        for b in range(4):
-            at = 3 - b + 4 * H * half
-            g.scalar.activation(T.ft[:, 4 * H * b:4 * H * b + 4 * H], T.diag[:, at:at + 4 * H], Copy).then_inc(S.ftd, 1)
-        g.vector.memset(T.h2[:, 4 * H:512], 0.0).then_inc(S.h2z, 1)
-    g.vector.wait_ge(S.dg, 1)
+    if rank:
+        g.sync.dma_start(T.bt[:], T.b[:]).then_inc(S.lb, 16)
+        g.sync.dma_start(T.at[:, 0:1536], T.a[:, 0:1536]).then_inc(S.la, 16)
+        g.sync.dma_start(T.at[:, 1536:2048], T.a[:, 1536:2048]).then_inc(S.la3, 16)
 
     def select(b):
         return g.vector.quantize_mx(T.eq[:, W * b:W * b + W], T.esc[:, W * b:W * b + W], T.diag[:, 3 - b:515 - b])
 
-    if give is not None:
-        select(give).then_inc(S.egd, 1)
-    for b in makes:
-        select(b).then_inc(S.eqd, 1)
-    if half is not None:
-        g.vector.wait_ge(S.ftd, 4)
-        g.vector.quantize_mx(T.fq[:], T.fsc[:], T.ft[:]).then_inc(S.fqd, 1)
-    g.vector.wait_ge(S.lb, 16)
-    g.vector.quantize_mx(T.bq[:], T.bsc[:], T.bt[:]).then_inc(S.bqd, 1)
-    g.vector.wait_ge(S.la, 16)
-    for i in range(4):
-        if i == 3:
-            g.vector.wait_ge(S.la3, 16)
-        g.vector.quantize_mx(T.aq[:, W * i:W * i + W], T.asc[:, W * i:W * i + W],
-                             T.at[:, 512 * i:512 * i + 512]).then_inc(S["aq%d" % i], 1)
+    if rank or give is not None:
+        g.vector.memset(T.ones[:], 1.0).then_inc(S.one, 1)
+        g.wait_ge(S.one, 1)
+        g.affine_select(T.diag[:], T.ones[:], [[1, 516]], AluOpType.is_equal, 0.0, -3, -4).then_inc(S.dg, 1)
+        if half is not None:
+            g.scalar.wait_ge(S.dg, 1)
+            for b in range(4):
+                at = 3 - b + 4 * H * half
+                g.scalar.activation(T.ft[:, 4 * H * b:4 * H * b + 4 * H], T.diag[:, at:at + 4 * H], Copy).then_inc(S.ftd, 1)
+            g.vector.memset(T.h2[:, 4 * H:512], 0.0).then_inc(S.h2z, 1)
+        g.vector.wait_ge(S.dg, 1)
+        if give is not None:
+            select(give).then_inc(S.egd, 1)
+        for b in makes:
+            select(b).then_inc(S.eqd, 1)
+    if rank:
+        g.vector.wait_ge(S.lb, 16)
+        g.vector.quantize_mx(T.bq[:], T.bsc[:], T.bt[:]).then_inc(S.bqd, 1)
+        g.vector.wait_ge(S.la, 16)
+        for i in range(4):
+            if i == 3:
+                g.vector.wait_ge(S.la3, 16)
+            g.vector.quantize_mx(T.aq[:, W * i:W * i + W], T.asc[:, W * i:W * i + W],
+                                 T.at[:, 512 * i:512 * i + 512]).then_inc(S["aq%d" % i], 1)
 
     def product(bank, i, start, stop):
         return g.tensor.matmul_mx(bank[:, 512 * i:512 * i + W], T.aq[:, W * i:W * i + W], T.asc[:, W * i:W * i + W],
@@ -175,12 +190,13 @@ def rank_program(g, core, T, topo):
             g.tensor.wait_ge(S["c_" + s], need(s, "c"))
             g.tensor.wait_ge(S["s_" + s], need(s, "s"))
 
-    g.tensor.wait_ge(S.bqd, 1)
-    for i in range(4):
-        g.tensor.wait_ge(S["aq%d" % i], 1)
-        product(T.acc, i, True, True).then_inc(S["pr%d" % i], 1)
-    for i in range(4):
-        product(T.tot, i, True, False)
+    if rank:
+        g.tensor.wait_ge(S.bqd, 1)
+        for i in range(4):
+            g.tensor.wait_ge(S["aq%d" % i], 1)
+            product(T.acc, i, True, True).then_inc(S["pr%d" % i], 1)
+        for i in range(4):
+            product(T.tot, i, True, False)
     if half is not None:
         g.tensor.wait_ge(S.fqd, 1)
         g.tensor.wait_ge(S.t1, 1)
@@ -193,7 +209,8 @@ def rank_program(g, core, T, topo):
                                        slot == "OWN", slot == mates[-1])
                 if slot == mates[-1]:
                     u.then_inc(S["su%d" % k], 1)
-    g.tensor.wait_ge(S.eqd, len(makes))
+    if rank:
+        g.tensor.wait_ge(S.eqd, len(makes))
     if give is not None:
         g.tensor.wait_ge(S.egd, 1)
     for slot in gets:
@@ -201,8 +218,7 @@ def rank_program(g, core, T, topo):
     for slot in total:
         if half is None or slot not in mates:
             arrive(slot)
-        q, p = ("lq_" + slot), ("lp_" + slot)
-        q, p = T[q][:], T[p][:]
+        q, p = T["lq_" + slot][:], T["lp_" + slot][:]
         for b in range(4):
             out = T.tot[:, 512 * b:512 * b + W]
             e, x = T.eq[:, W * b:W * b + W], T.esc[:, W * b:W * b + W]
@@ -213,15 +229,24 @@ def rank_program(g, core, T, topo):
             if slot == total[-1]:
                 u.then_inc(S["yb%d" % b], 1)
 
-    for b in range(3):
-        g.scalar.wait_ge(S["pr%d" % b], 1)
-        g.scalar.activation(T.h1[:, b:512:4], T.acc[:, 512 * b:512 * b + W], Copy).then_inc(S.h1d, 1)
-    g.vector.wait_ge(S.pr3, 1)
-    g.vector.tensor_copy(T.h1[:, 3:512:4], T.acc[:, 1536:1536 + W]).then_inc(S.h1d, 1)
-    g.vector.wait_ge(S.h1d, 4)
-    g.vector.quantize_mx(T.q1[:], T.p1[:], T.h1[:]).then_inc(S.t1, 1)
+    def bank_copy(b, sem, bank, tile, done):
+        src, dst = bank[:, 512 * b:512 * b + W], tile[:, b:512:4]
+        if b % 2 == 0:
+            g.scalar.wait_ge(sem, 1)
+            g.scalar.activation(dst, src, Copy).then_inc(done, 1)
+        else:
+            g.vector.wait_ge(sem, 1)
+            g.vector.tensor_copy(dst, src).then_inc(done, 1)
+
+    if rank:
+        for b in range(4):
+            bank_copy(b, S["pr%d" % b], T.acc, T.h1, S.h1d)
+        g.vector.wait_ge(S.h1d, 4)
+        g.vector.quantize_mx(T.q1[:], T.p1[:], T.h1[:]).then_inc(S.t1, 1)
 
     if half is not None:
+        g.vector.wait_ge(S.ftd, 4)
+        g.vector.quantize_mx(T.fq[:], T.fsc[:], T.ft[:]).then_inc(S.fqd, 1)
         g.scalar.wait_ge(S.su0, 1)
         for b in (0, 1):
             g.scalar.activation(T.h2[:, b:4 * H:4], T.acc[:, H * b:H * b + H], Copy).then_inc(S.h2d, 1)
@@ -232,31 +257,26 @@ def rank_program(g, core, T, topo):
         g.vector.wait_ge(S.h2d, 4)
         g.vector.quantize_mx(T.q2[:], T.p2[:], T.h2[:]).then_inc(S.t2, 1)
 
-    for b in range(4):
-        src, dst = T.tot[:, 512 * b:512 * b + W], T.yt[:, b:512:4]
-        if b % 2 == 0:
-            g.scalar.wait_ge(S["yb%d" % b], 1)
-            g.scalar.activation(dst, src, Copy).then_inc(S.ycp, 1)
-        else:
-            g.vector.wait_ge(S["yb%d" % b], 1)
-            g.vector.tensor_copy(dst, src).then_inc(S.ycp, 1)
-    g.sync.wait_ge(S.ycp, 4)
-    g.sync.dma_start(T.y[:], T.yt[:]).then_inc(S.yst, 16)
-    g.sync.wait_ge(S.yst, 16)
+    if rank:
+        for b in range(4):
+            bank_copy(b, S["yb%d" % b], T.tot, T.yt, S.ycp)
+        g.sync.wait_ge(S.ycp, 4)
+        g.sync.dma_start(T.y[:], T.yt[:]).then_inc(S.yst, 16)
+        g.sync.wait_ge(S.yst, 16)
 
     seen, sent = [], 0
     for src, dsts, slot, part, what, mask, n in R:
         if src != core:
             continue
-        lo, hi, ql, pl = 0, W, "lq_" + slot, "lp_" + slot
-        if slot[0] == "S":
-            lo = H * int(slot[1])
-            hi, ql, pl = lo + H, "lq_S", "lp_S"
         if what == "E":
             key, sem, val = what, S.egd, 1
             q, p = T.eq[:, W * give:W * give + W], T.esc[:, W * give:W * give + W]
             q_out, p_out = q, p
         else:
+            lo, hi, ql, pl = 0, W, "lq_" + slot, "lp_" + slot
+            if slot[0] == "S":
+                lo = H * int(slot[1])
+                hi, ql, pl = lo + H, "lq_S", "lp_S"
             q_out, p_out = T[ql][:, lo:hi], T[pl][:, lo:hi]
             if what in ("1", "2"):
                 key, sem, val = what, S["t" + what], 1

from concourse.bass import DstId, RemoteDMATransfer
from concourse.mybir import dt, AluOpType, ActivationFunctionType

W = 128
H = 64
WORLD = 512
SLOTS = ["M0", "M1", "M2", "M3", "M4", "NEAR", "CAB", "FAR"]
HUBS = [0, 2]
SENDS = {0: [2, 1, 3, 4], 2: [0, 3, 4, 1], 1: [0, 2, 4, 3], 4: [0, 2, 3, 1], 3: [2, 0, 1, 4]}
LAND = {"NEARc": 1, "NEARs": 4, "CABc": 7, "CABs": 3, "FARc": 3, "FARs": 4}
AWAY_FIRST = ("CABc", "CABs", "NEARs")
TO = {0: 1, 1: 4, 4: 0, 2: 3, 3: 2}
GIVES = {0: 0, 1: 1, 4: 2, 2: 0, 3: 1}
BF, F8, U8 = "bfloat16", "float8_e4m3fn_x4", "uint8"
SCRATCH = {"acc": ("psum", [128, 2048], "float32"), "tot": ("psum", [128, 2048], "float32"), "yt": ("sbuf", [128, 512], "float32")}
for _n, _w, _d in (("at", 2048, BF), ("bt", 512, BF), ("ones", 516, BF), ("diag", 516, BF), ("ft", 1024, BF), ("h1", 512, BF), ("h2", 512, BF),
                   ("aq", 512, F8), ("asc", 512, U8), ("bq", 128, F8), ("bsc", 128, U8), ("eq", 512, F8), ("esc", 512, U8),
                   ("fq", 256, F8), ("fsc", 256, U8), ("q1", 128, F8), ("p1", 128, U8), ("q2", 128, F8), ("p2", 128, U8)):
    SCRATCH[_n] = ("sbuf", [128, _w], _d)
for _s in SLOTS + ["S"]:
    SCRATCH["lq_" + _s] = ("sbuf", [128, 128], F8)
    SCRATCH["lp_" + _s] = ("sbuf", [128, 128], U8)
SEMAPHORES = (["lb", "la", "la3", "one", "dg", "eqd", "egd", "ftd", "fqd", "bqd", "h1d", "t1", "h2z", "h2d", "t2", "ycp", "yst", "sent",
               "su0", "su1"]
              + ["aq%d" % i for i in range(4)] + ["pr%d" % i for i in range(4)] + ["yb%d" % i for i in range(4)]
              + [p + s for p in ("c_", "s_") for s in SLOTS + ["S0", "S1", "E0", "E1", "E2", "E3"]])


def roles(T, topo):
    hosts = {}
    for c in T.cores:
        hosts.setdefault(topo.host(c), []).append(c)
    team = max(hosts.values(), key=len)
    near = cab = far = None
    for c in T.cores:
        if c in team:
            continue
        if not topo.may_write(team[0], c):
            far = c
        elif topo.rack(topo.host(c)) == topo.rack(topo.host(team[0])):
            near = c
        else:
            cab = c
    return team, near, cab, far


def helpers(T, topo, team, near, cab):
    def free(x):
        return [c for c in range(WORLD) if topo.host(c) == topo.host(x) and topo.chip(c) == topo.chip(x) and T.rank_of(c) is None]
    return (free(team[0]), [c for c in free(near) if topo.die(c) != topo.die(near)][0],
            [c for c in free(cab) if topo.die(c) != topo.die(cab)][0])


def engines(topo, src, dsts, k):
    m = -1
    for d in dsts:
        m &= topo.mask(src, d)
    es = [e for e in range(m.bit_length()) if m >> e & 1]
    es = es[:k] if k > 0 else es[k:]
    return sum(1 << e for e in es), len(es)


def routes(T, topo):
    team, near, cab, far = roles(T, topo)
    extra, nh, ch = helpers(T, topo, team, near, cab)
    hubs = [team[i] for i in HUBS]
    rest = [c for c in team if c not in hubs]
    at = {k: (team + extra)[v] for k, v in LAND.items()}
    R = []

    def add(src, dsts, slot, parts, what, k):
        for p in parts:
            mask, n = engines(topo, src, dsts, k)
            R.append((src, list(dsts), slot, p, what, mask, n))

    add(extra[0], hubs, "E3", "cs", "E", 16)
    add(extra[1], rest[:1], "E3", "cs", "E", 16)
    add(extra[2], rest[1:], "E3", "cs", "E", 16)
    add(nh, [near], "E3", "cs", "E", 16)
    add(ch, [cab], "E3", "cs", "E", 16)
    for i in range(5):
        add(team[i], [team[TO[i]]], "E%d" % GIVES[i], "cs", "E", 16)
    for i in range(5):
        for d in SENDS[i]:
            add(team[i], [team[d]], "M%d" % i, "cs", "1", 16)
    for h, first, then, slot in ((hubs[0], near, cab, "S0"), (hubs[1], cab, near, "S1")):
        add(h, [first], slot, "cs", "2", 8)
        add(h, [then], slot, "cs", "2", 8)
    for m, slot in ((near, "NEAR"), (cab, "CAB")):
        add(m, [at[slot + "c"]], slot, "c", "1", 8)
        add(m, [at[slot + "s"]], slot, "s", "1", 8)
        add(m, [far], slot, "cs", "1", 8)
    add(far, [ch], "FAR", "c", "1", 8)
    add(far, [nh], "FAR", "s", "1", 8)
    add(far, [near], "FAR", "c", "1", 8)
    add(far, [cab], "FAR", "s", "1", 8)
    for m, lone, part in ((ch, cab, "c"), (nh, near, "s")):
        add(m, [at["FAR" + part]], "FAR", part, "FAR", 8)
        add(m, [lone], "FAR", part, "FAR", -8)
    add(near, [far], "S0", "cs", "S0", 8)
    add(cab, [far], "S1", "cs", "S1", 8)
    for slot, part, away in (("NEAR", "c", cab), ("CAB", "c", near), ("NEAR", "s", cab), ("CAB", "s", near),
                             ("FAR", "c", None), ("FAR", "s", None)):
        m = at[slot + part]
        if slot + part in AWAY_FIRST:
            add(m, [away], slot, part, slot, 8)
        for same in (False, True):
            ds = [d for d in team if d != m and (topo.die(d) == topo.die(m)) == same]
            if ds:
                add(m, ds, slot, part, slot, 16)
        if away is not None and slot + part not in AWAY_FIRST:
            add(m, [away], slot, part, slot, 8)
    return R


def rank_program(g, core, T, topo):
    rank = T.rank_of(core) is not None
    if not any(topo.host(c) == topo.host(core) and topo.chip(c) == topo.chip(core) for c in T.cores):
        return
    team, near, cab, far = roles(T, topo)
    R = routes(T, topo)
    if not any(core == r[0] or core in r[1] for r in R):
        return
    half = None
    for k, i in enumerate(HUBS):
        if team[i] == core:
            half = k
    S = T.sem
    Copy = ActivationFunctionType.Copy

    def need(slot, part):
        return [r[6] for r in R if core in r[1] and r[2] == slot and r[3] == part][0]

    mates, total = [], []
    if core in team:
        me = team.index(core)
        mates = ["M%d" % i for _, i in sorted([(SENDS[i].index(me), i) for i in SENDS if i != me])]
        total = mates + ["NEAR", "CAB", "FAR"]
    elif rank:
        total = [s for s, own in (("FAR", far), ("NEAR", near), ("CAB", cab)) if own != core] + ["S"]

    gets = [r[2] for r in R if core in r[1] and r[4] == "E" and r[3] == "c"]
    makes = [b for b in range(4) if "E%d" % b not in gets] if rank else []
    give = None
    for r in R:
        if r[0] == core and r[4] == "E":
            give = int(r[2][1])
    if give in makes:
        makes.remove(give)

    if rank:
        g.sync.dma_start(T.bt[:], T.b[:]).then_inc(S.lb, 16)
        g.sync.dma_start(T.at[:, 0:1536], T.a[:, 0:1536]).then_inc(S.la, 16)
        g.sync.dma_start(T.at[:, 1536:2048], T.a[:, 1536:2048]).then_inc(S.la3, 16)

    def select(b):
        return g.vector.quantize_mx(T.eq[:, W * b:W * b + W], T.esc[:, W * b:W * b + W], T.diag[:, 3 - b:515 - b])

    if rank or give is not None:
        g.vector.memset(T.ones[:], 1.0).then_inc(S.one, 1)
        g.wait_ge(S.one, 1)
        g.affine_select(T.diag[:], T.ones[:], [[1, 516]], AluOpType.is_equal, 0.0, -3, -4).then_inc(S.dg, 1)
        if half is not None:
            g.scalar.wait_ge(S.dg, 1)
            for b in range(4):
                at = 3 - b + 4 * H * half
                g.scalar.activation(T.ft[:, 4 * H * b:4 * H * b + 4 * H], T.diag[:, at:at + 4 * H], Copy).then_inc(S.ftd, 1)
            g.vector.memset(T.h2[:, 4 * H:512], 0.0).then_inc(S.h2z, 1)
        g.vector.wait_ge(S.dg, 1)
        if give is not None:
            select(give).then_inc(S.egd, 1)
        for b in makes:
            select(b).then_inc(S.eqd, 1)
    if rank:
        g.vector.wait_ge(S.lb, 16)
        g.vector.quantize_mx(T.bq[:], T.bsc[:], T.bt[:]).then_inc(S.bqd, 1)
        g.vector.wait_ge(S.la, 16)
        for i in range(4):
            if i == 3:
                g.vector.wait_ge(S.la3, 16)
            g.vector.quantize_mx(T.aq[:, W * i:W * i + W], T.asc[:, W * i:W * i + W],
                                 T.at[:, 512 * i:512 * i + 512]).then_inc(S["aq%d" % i], 1)

    def product(bank, i, start, stop):
        return g.tensor.matmul_mx(bank[:, 512 * i:512 * i + W], T.aq[:, W * i:W * i + W], T.asc[:, W * i:W * i + W],
                                  T.bq[:], T.bsc[:], start, stop)

    def arrive(slot):
        for s in (["S0", "S1"] if slot == "S" else [slot]):
            g.tensor.wait_ge(S["c_" + s], need(s, "c"))
            g.tensor.wait_ge(S["s_" + s], need(s, "s"))

    if rank:
        g.tensor.wait_ge(S.bqd, 1)
        for i in range(4):
            g.tensor.wait_ge(S["aq%d" % i], 1)
            product(T.acc, i, True, True).then_inc(S["pr%d" % i], 1)
        for i in range(4):
            product(T.tot, i, True, False)
    if half is not None:
        g.tensor.wait_ge(S.fqd, 1)
        g.tensor.wait_ge(S.t1, 1)
        for slot in ["OWN"] + mates:
            if slot != "OWN":
                arrive(slot)
            q, p = (T.q1, T.p1) if slot == "OWN" else (T["lq_" + slot], T["lp_" + slot])
            for k in range(2):
                u = g.tensor.matmul_mx(T.acc[:, 512 * k:512 * k + W], q[:], p[:], T.fq[:, W * k:W * k + W], T.fsc[:, W * k:W * k + W],
                                       slot == "OWN", slot == mates[-1])
                if slot == mates[-1]:
                    u.then_inc(S["su%d" % k], 1)
    if rank:
        g.tensor.wait_ge(S.eqd, len(makes))
    if give is not None:
        g.tensor.wait_ge(S.egd, 1)
    for slot in gets:
        arrive(slot)
    for slot in total:
        if half is None or slot not in mates:
            arrive(slot)
        q, p = T["lq_" + slot][:], T["lp_" + slot][:]
        for b in range(4):
            out = T.tot[:, 512 * b:512 * b + W]
            e, x = T.eq[:, W * b:W * b + W], T.esc[:, W * b:W * b + W]
            if slot == "S":
                u = g.tensor.matmul_mx(out, q, p, e, x, False, slot == total[-1])
            else:
                u = g.tensor.matmul_mx(out, e, x, q, p, False, slot == total[-1])
            if slot == total[-1]:
                u.then_inc(S["yb%d" % b], 1)

    def bank_copy(b, sem, bank, tile, done):
        src, dst = bank[:, 512 * b:512 * b + W], tile[:, b:512:4]
        if b % 2 == 0:
            g.scalar.wait_ge(sem, 1)
            g.scalar.activation(dst, src, Copy).then_inc(done, 1)
        else:
            g.vector.wait_ge(sem, 1)
            g.vector.tensor_copy(dst, src).then_inc(done, 1)

    if rank:
        for b in range(4):
            bank_copy(b, S["pr%d" % b], T.acc, T.h1, S.h1d)
        g.vector.wait_ge(S.h1d, 4)
        g.vector.quantize_mx(T.q1[:], T.p1[:], T.h1[:]).then_inc(S.t1, 1)

    if half is not None:
        g.vector.wait_ge(S.ftd, 4)
        g.vector.quantize_mx(T.fq[:], T.fsc[:], T.ft[:]).then_inc(S.fqd, 1)
        g.scalar.wait_ge(S.su0, 1)
        for b in (0, 1):
            g.scalar.activation(T.h2[:, b:4 * H:4], T.acc[:, H * b:H * b + H], Copy).then_inc(S.h2d, 1)
        g.vector.wait_ge(S.su1, 1)
        for b in (2, 3):
            g.vector.tensor_copy(T.h2[:, b:4 * H:4], T.acc[:, 512 + H * (b - 2):512 + H * (b - 2) + H]).then_inc(S.h2d, 1)
        g.vector.wait_ge(S.h2z, 1)
        g.vector.wait_ge(S.h2d, 4)
        g.vector.quantize_mx(T.q2[:], T.p2[:], T.h2[:]).then_inc(S.t2, 1)

    if rank:
        for b in range(4):
            bank_copy(b, S["yb%d" % b], T.tot, T.yt, S.ycp)
        g.sync.wait_ge(S.ycp, 4)
        g.sync.dma_start(T.y[:], T.yt[:]).then_inc(S.yst, 16)
        g.sync.wait_ge(S.yst, 16)

    seen, sent = [], 0
    for src, dsts, slot, part, what, mask, n in R:
        if src != core:
            continue
        if what == "E":
            key, sem, val = what, S.egd, 1
            q, p = T.eq[:, W * give:W * give + W], T.esc[:, W * give:W * give + W]
            q_out, p_out = q, p
        else:
            lo, hi, ql, pl = 0, W, "lq_" + slot, "lp_" + slot
            if slot[0] == "S":
                lo = H * int(slot[1])
                hi, ql, pl = lo + H, "lq_S", "lp_S"
            q_out, p_out = T[ql][:, lo:hi], T[pl][:, lo:hi]
            if what in ("1", "2"):
                key, sem, val = what, S["t" + what], 1
                q, p = T["q" + what][:, 0:hi - lo], T["p" + what][:, 0:hi - lo]
            else:
                key, sem, val = what + part, S[part + "_" + what], need(what, part)
                q, p = q_out, p_out
        if key not in seen:
            seen.append(key)
            g.wait_ge(sem, val)
        if part == "c":
            ap_in, ap_out = q.bitcast(dt.uint8), q_out.bitcast(dt.uint8)
        else:
            ap_in, ap_out = p, p_out
        if len(dsts) == 1:
            rid, pid = topo.addr(dsts[0], core)
            g.remote_dma(out_ap=ap_out, in_ap=ap_in, remote_sem=S[part + "_" + slot], local_sem=S.sent, pid=pid,
                         routing_id=rid, dma_engine_mask=mask)
        else:
            ids = []
            for d in dsts:
                rid, pid = topo.addr(d, core)
                ids.append(DstId(rid=rid, pnc=pid))
            g.remote_dma_fused([RemoteDMATransfer(dst_ids=ids, dma_engine_mask=mask, remote_sem=S[part + "_" + slot],
                                                  srcs=[ap_in], dsts=[ap_out for _ in dsts], alu_op=0)], local_sem=S.sent)
        sent += n
    g.wait_ge(S.sent, sent)
